import numpy as np
import ml_dtypes


def mxq(x, axis, fmt="e4m3"):
    dtype, down = {"e4m3": (ml_dtypes.float8_e4m3fn, 7), "e5m2": (ml_dtypes.float8_e5m2, 14)}[fmt]
    v = np.moveaxis(np.asarray(x, np.float32).astype(ml_dtypes.bfloat16).astype(np.float64), axis, -1)
    blocks = v.reshape(v.shape[:-1] + (-1, 32))
    amax = np.abs(blocks).max(-1, keepdims=True)
    byte = np.maximum(np.where(amax > 0, np.frexp(amax)[1] - 1 + 127, 0) - down, 1)
    scale = np.exp2(byte - 127.0)
    codes = (blocks / scale).astype(np.float32).astype(dtype).astype(np.float64)
    return np.moveaxis((codes * scale).reshape(v.shape), -1, axis)


WIDE = False


def mx_kscale(k):
    if not WIDE:
        return np.ones(k)
    levels = np.array([10, -10, 5, -5, 0])
    if k % 512:
        return np.exp2(np.random.permutation(np.resize(levels, k // 32))).repeat(32)
    a = np.empty((k // 512, 16))
    for p in range(k // 512):
        a[p, :8] = np.random.permutation(np.resize(levels, 8))
        for g in range(8):
            far = levels[np.abs(levels - a[p, g]) >= 10]
            a[p, g + 8] = far[np.random.randint(len(far))]
    return np.exp2(a.ravel()).repeat(32)


def f64(x):
    return np.asarray(x).astype(np.float64)


def striped(idx):
    return np.tile(idx.reshape(-1, 16).T, (8, 1)).astype(np.uint16)


def unstriped(offs):
    return offs[:16].T.reshape(-1).astype(np.int64)


def striped8(idx):
    return np.concatenate([x.reshape(-1, 16).T for x in idx]).astype(np.uint16)


def runs(offs, k):
    lists = np.stack([offs[16 * r : 16 * r + 16].T.reshape(-1) for r in range(8)]).astype(np.int64)
    return lists[np.arange(k) % 512 // 64]


def pack_weight(w):
    k, n = w.shape
    w = f64(np.asarray(w, np.float32).astype(ml_dtypes.bfloat16)).reshape(k // 32, 32, n)
    amax = np.abs(w).max(1)
    byte = np.clip(np.where(amax > 0, np.frexp(amax)[1] - 1 + 127 - 7, 1), 1, 254)
    scaled = (w * np.exp2(127.0 - byte)[:, None, :]).reshape(k, n).astype(np.float32)
    words = np.ascontiguousarray(scaled.reshape(k // 512, 128, 4, n).transpose(0, 1, 3, 2)).astype(ml_dtypes.float8_e4m3fn).view(np.uint8)
    return words, np.ascontiguousarray(byte.astype(np.uint8).reshape(k // 512, 16, n))


def unpack_weight(words, scales):
    g, p, n, _ = words.shape
    vals = np.ascontiguousarray(words).view(ml_dtypes.float8_e4m3fn).astype(np.float64) * np.repeat(np.exp2(scales.astype(np.float64) - 127.0), 8, axis=1)[..., None]
    return vals.transpose(0, 1, 3, 2).reshape(g * 512, n)


K, T, S, N, H, G = 512, 2048, 256, 512, 512, 2048


def setup_inputs():
    n = np.random.standard_normal
    s = mx_kscale(K)[:, None]
    u = mx_kscale(K)
    packed_xT = pack_weight(n((K, T)) * s)
    packed_dT = pack_weight(n((K, G)) / s)
    return {
        "x_words": packed_xT[0],
        "x_scales": packed_xT[1],
        "w1": (n((K, H)) / np.sqrt(K) / s).astype(np.float32),
        "gn": (np.random.uniform(0.5, 1.5, (H, 1)) * u[:, None]).astype(np.float32),
        "w2": (n((H, N)) / np.sqrt(H) / u[:, None]).astype(np.float32),
        "d_words": packed_dT[0],
        "d_scales": packed_dT[1],
        "tau": np.random.uniform(0.3, 0.9, (H, 1)).astype(np.float32),
        "offs": striped(np.random.permutation(T)[:S]),
        "n1": striped(np.random.permutation(S)),
        "n2": striped(np.random.permutation(S)),
        "two": striped(np.random.permutation(T)[:S]),
        "k1": striped8(np.random.randint(0, G, (8, H))),
        "n3": striped8(np.stack([np.random.permutation(S) for _ in range(8)])),
        "n4": striped8(np.stack([np.random.permutation(S) for _ in range(8)])),
    }


def reference(x_words, x_scales, w1, gn, w2, d_words, d_scales, tau, offs, n1, n2, two, k1, n3, n4):
    d_k1 = unpack_weight(d_words, d_scales)[np.arange(K)[:, None], runs(k1, K)]
    x_two = unpack_weight(x_words, x_scales)[:, unstriped(two)]
    b = 0.0625 * (d_k1.T @ x_two)
    top = b.max(axis=1, keepdims=True)
    ea = np.exp(f64(tau) * (b[np.arange(H)[:, None], runs(n3, H)] - top))
    xq = unpack_weight(x_words, x_scales)[:, unstriped(offs)]
    y = mxq(f64(w1), 0, "e4m3").T @ xq
    pa = y[:, unstriped(n1)]
    pb = y[:, unstriped(n2)]
    z = f64(gn) * (np.maximum(np.maximum(y, pa), pb) - (0.5 * (np.minimum(np.minimum(y, pa), pb))))
    a = mxq(f64(w2), 0, "e4m3").T @ mxq(z, 0, "e4m3")
    return (2.0 * ea) * (a - (a[np.arange(N)[:, None], runs(n4, N)])) - (0.5 * b)

@@ -1,0 +1,184 @@
+from contextlib import ExitStack
+
+import concourse.mybir as mybir
+
+F32 = mybir.dt.float32
+BF16 = mybir.dt.bfloat16
+I32 = mybir.dt.int32
+U32 = mybir.dt.uint32
+U16 = mybir.dt.uint16
+U8 = mybir.dt.uint8
+FP8X4 = mybir.dt.float8_e4m3fn_x4
+ALU = mybir.AluOpType
+ACT = mybir.ActivationFunctionType
+
+P = 128
+PACK = 4
+K = 512
+H = 512
+S = 256
+T = 2048
+WINDOW_EIGHT = 512
+WINDOW_ONE = 352
+FLOPS = 3 * 2 * K * H * S
+
+
+def tile_picked_cdjoinpxbrange_none_p_kernel(tc, x_words, x_scales, w1, gn, w2, d_words, d_scales, tau, offs, n1, n2, two, k1, n3, n4, out):
+    nc = tc.nc
+    with ExitStack() as ctx:
+        lists = ctx.enter_context(tc.tile_pool(name="lists", bufs=1))
+        sb = ctx.enter_context(tc.tile_pool(name="sb", bufs=1))
+        psum = ctx.enter_context(tc.psum_pool(name="psum", bufs=1))
+
+        def load_list(name, src):
+            tile = lists.tile([P, src.shape[1]], U16, name=name)
+            nc.sync.dma_start(tile[:], src)
+            return tile
+
+        def load_weight_half(name, w, half, queue):
+            tile = sb.tile([P, PACK, H // 2], F32, name=name)
+            cols = slice(half * H // 2, (half + 1) * H // 2)
+            queue.dma_start(tile[:], w.rearrange("(p j) c -> p j c", j=PACK)[:, :, cols])
+            return tile
+
+        def load_words(name, words, queue):
+            tile = sb.tile([P, T], U32, name=name)
+            queue.dma_start(tile[:].bitcast(I32), words[0].rearrange("p n r -> p (n r)").bitcast(I32))
+            return tile
+
+        x_bytes = sb.tile([P, T], U8, name="x_bytes")
+        d_bytes = sb.tile([P, T], U8, name="d_bytes")
+        d_plane = sb.tile([P, H], U8, name="d_plane", align_bytes=64)
+        for tile in (x_bytes, d_bytes, d_plane):
+            nc.vector.memset(tile[:].bitcast(I32), 0)
+
+        offs_sb = load_list("offs_sb", offs)
+        k1_sb = load_list("k1_sb", k1)
+        two_sb = load_list("two_sb", two)
+        n1_sb = load_list("n1_sb", n1)
+        n2_sb = load_list("n2_sb", n2)
+        n3_sb = load_list("n3_sb", n3)
+        n4_sb = load_list("n4_sb", n4)
+        w1_raw = [load_weight_half("w_raw%d" % half, w1, half, nc.sync) for half in range(2)]
+        x_table = load_words("x_table", x_words, nc.sync)
+        d_table = load_words("d_table", d_words, nc.sync)
+        for j in range(PACK):
+            nc.scalar.dma_start(x_bytes[j:P:32, :].bitcast(I32), x_scales[0, j:16:PACK, :].bitcast(I32))
+        nc.scalar.dma_start(d_bytes[0:P:8, :].bitcast(I32), d_scales[0].bitcast(I32))
+        gn_sb = sb.tile([P, PACK], F32, name="gn_sb")
+        tau_sb = sb.tile([P, PACK], F32, name="tau_sb")
+        nc.gpsimd.dma_start(gn_sb[:], gn.rearrange("(p t) o -> p (t o)", t=PACK))
+        nc.gpsimd.dma_start(tau_sb[:], tau.rearrange("(p t) o -> p (t o)", t=PACK))
+
+        y_win = [sb.tile([P, WINDOW_ONE], F32, name="y_win%d" % t) for t in range(PACK)]
+        b_win = [sb.tile([P, WINDOW_EIGHT], F32, name="b_win%d" % t) for t in range(PACK)]
+        a_win = [sb.tile([P, WINDOW_EIGHT], F32, name="a_win%d" % t) for t in range(PACK)]
+        for tile in y_win + b_win + a_win:
+            nc.vector.memset(tile[:, S:], 0.0)
+
+        def gather_packed(name, table, offsets, dtype):
+            tile = sb.tile([P, 16 * offsets.shape[1]], dtype, name=name, align_bytes=64)
+            nc.vector.tensor_copy(tile[:], table[:].indirect(offsets[:]))
+            return tile
+
+        def deal(name, picked, dtype):
+            tile = sb.tile([P, H], dtype, name=name, align_bytes=64)
+            nc.vector.tensor_copy(
+                tile[:].rearrange("p (t m) -> p m t", t=PACK), picked[:].rearrange("p (m t) -> p m t", t=PACK)
+            )
+            return tile
+
+        def round_weight_half(copy, grouped, raw, half):
+            m_half = slice(half * P // 2, (half + 1) * P // 2)
+            copy(
+                grouped[:].rearrange("p (t m j) -> p m j t", t=PACK, j=PACK)[:, m_half],
+                raw[:].rearrange("p j (m t) -> p m j t", t=PACK),
+            )
+
+        def quantise(name, grouped, width):
+            codes = sb.tile([P, width], U32, name=name + "_codes", align_bytes=64)
+            plane = sb.tile([P, width], U8, name=name + "_plane", align_bytes=64)
+            nc.vector.quantize_mx(codes[:].bitcast(FP8X4), plane[:], grouped[:])
+            return codes, plane
+
+        def product(acc, codes, plane, t, rhs_codes, rhs_plane):
+            cols = slice(t * P, (t + 1) * P)
+            nc.tensor.matmul_mx(acc, lhsT=codes[:, cols].bitcast(FP8X4), lhsT_scale=plane[:, cols],
+                                rhs=rhs_codes[:].bitcast(FP8X4), rhs_scale=rhs_plane[:], start=True, stop=True)
+
+        xq_plane = gather_packed("xq_plane", x_bytes, offs_sb, U8)
+        dk_bytes = gather_packed("dk_bytes", d_bytes, k1_sb, U8)
+        dk_dealt = deal("dk_dealt", dk_bytes, U8)
+        for j in range(PACK):
+            nc.sync.dma_start(d_plane[j:P:32, :].bitcast(I32), dk_dealt[8 * j:P:32, :].bitcast(I32))
+        xt_plane = gather_packed("xt_plane", x_bytes, two_sb, U8)
+
+        w1_grouped = sb.tile([P, PACK * H], BF16, name="w1_grouped", align_bytes=64)
+        round_weight_half(nc.scalar.copy, w1_grouped, w1_raw[0], 0)
+        round_weight_half(nc.scalar.copy, w1_grouped, w1_raw[1], 1)
+        w2_raw = [load_weight_half("w_raw%d" % half, w2, half, nc.sync) for half in range(2)]
+        w1_codes, w1_plane = quantise("w1", w1_grouped, H)
+        xq_codes = gather_packed("xq_codes", x_table, offs_sb, U32)
+
+        y_bank = [psum.tile([P, 2, S], F32, name="y_bank%d" % u) for u in range(2)]
+        for t in range(PACK):
+            product(y_bank[t // 2][:, t % 2, :], w1_codes, w1_plane, t, xq_codes, xq_plane)
+
+        xt_codes = gather_packed("xt_codes", x_table, two_sb, U32)
+        dk_words = gather_packed("dk_words", d_table, k1_sb, U32)
+        d_codes = deal("d_codes", dk_words, U32)
+        b_bank = [psum.tile([P, 2, S], F32, name="b_bank%d" % u) for u in range(2)]
+        for t in range(PACK):
+            product(b_bank[t // 2][:, t % 2, :], d_codes, d_plane, t, xt_codes, xt_plane)
+
+        pa = sb.tile([P, PACK, S], F32, name="pa")
+        pb = sb.tile([P, PACK, S], F32, name="pb")
+        hi = sb.tile([P, PACK, S], F32, name="hi")
+        lo = sb.tile([P, PACK, S], F32, name="lo")
+        z_rows = sb.tile([P, PACK, S], BF16, name="z_rows")
+        top = sb.tile([P, PACK], F32, name="top")
+        shift = sb.tile([P, PACK], F32, name="shift")
+        ea = sb.tile([P, PACK, S], F32, name="ea")
+        w2_grouped = sb.tile([P, PACK * H], BF16, name="w2_grouped", align_bytes=64)
+        for u in range(2):
+            pair = slice(2 * u, 2 * u + 2)
+            for t in range(2 * u, 2 * u + 2):
+                nc.scalar.copy(y_win[t][:, :S], y_bank[u][:, t % 2, :])
+                nc.scalar.activation(pa[:, t, :], y_win[t][:].indirect(n1_sb[:]), ACT.Copy)
+            for t in range(2 * u, 2 * u + 2):
+                nc.scalar.activation(pb[:, t, :], y_win[t][:].indirect(n2_sb[:]), ACT.Copy)
+            nc.vector.tensor_tensor(hi[:, pair, :], y_bank[u][:], pa[:, pair, :], ALU.max)
+            nc.vector.tensor_tensor(lo[:, pair, :], y_bank[u][:], pa[:, pair, :], ALU.min)
+            nc.vector.tensor_tensor(hi[:, pair, :], hi[:, pair, :], pb[:, pair, :], ALU.max)
+            nc.vector.tensor_tensor(lo[:, pair, :], lo[:, pair, :], pb[:, pair, :], ALU.min)
+            for t in range(2 * u, 2 * u + 2):
+                nc.vector.tensor_scalar(b_win[t][:, :S], b_bank[u][:, t % 2, :], 0.0625, None, ALU.mult, ALU.max,
+                                        accum_out=top[:, t:t + 1])
+            nc.vector.scalar_tensor_tensor(hi[:, pair, :], lo[:, pair, :], -0.5, hi[:, pair, :], ALU.mult, ALU.add)
+            nc.vector.scalar_tensor_tensor(shift[:, pair], top[:, pair], -1.0, tau_sb[:, pair], ALU.mult, ALU.mult)
+            for t in range(2 * u, 2 * u + 2):
+                nc.vector.tensor_scalar(z_rows[:, t, :], hi[:, t, :], gn_sb[:, t:t + 1], None, ALU.mult)
+        for half in range(2):
+            round_weight_half(nc.scalar.copy, w2_grouped, w2_raw[half], half)
+        w2_codes, w2_plane = quantise("w2", w2_grouped, H)
+        for t in range(PACK):
+            nc.scalar.activation(ea[:, t, :], b_win[t][:].indirect(n3_sb[:]), ACT.Exp,
+                                 bias=shift[:, t:t + 1], scale=tau_sb[:, t:t + 1])
+
+        z_grouped = sb.tile([P, S * PACK], BF16, name="z_grouped", align_bytes=64)
+        nc.vector.tensor_copy(z_grouped[:].rearrange("p (c i t) -> p c t i", i=4, t=PACK),
+                              z_rows[:].rearrange("p t (c i) -> p c t i", i=4))
+        z_codes, z_plane = quantise("z", z_grouped, S)
+
+        out_rows = out.rearrange("(p t) c -> p t c", t=PACK)
+        for t in range(PACK):
+            a_bank = psum.tile([P, S], F32, name="a_bank%d" % t)
+            product(a_bank[:], w2_codes, w2_plane, t, z_codes, z_plane)
+            nc.scalar.copy(a_win[t][:, :S], a_bank[:])
+            fetched = sb.tile([P, S], F32, name="fetched%d" % t)
+            nc.scalar.activation(fetched[:], a_win[t][:].indirect(n4_sb[:]), ACT.Copy)
+            result = sb.tile([P, S], F32, name="result%d" % t)
+            nc.vector.tensor_tensor(result[:], a_win[t][:, :S], fetched[:], ALU.subtract)
+            nc.vector.scalar_tensor_tensor(result[:], result[:], 2.0, ea[:, t, :], ALU.mult, ALU.mult)
+            nc.vector.scalar_tensor_tensor(result[:], b_win[t][:, :S], -0.5, result[:], ALU.mult, ALU.add)
+            nc.sync.dma_start(out_rows[:, t, :], result[:])

@@ -19,7 +19,7 @@ H = 512
 S = 256
 T = 2048
 WINDOW_EIGHT = 512
-WINDOW_ONE = 352
+WINDOW_ONE = 272
 FLOPS = 3 * 2 * K * H * S
 
 
@@ -42,29 +42,25 @@ def tile_picked_cdjoinpxbrange_none_p_kernel(tc, x_words, x_scales, w1, gn, w2, 
             return tile
 
         def load_words(name, words, queue):
-            tile = sb.tile([P, T], U32, name=name)
+            tile = sb.tile([P, T], U32, name=name, align_bytes=64)
             queue.dma_start(tile[:].bitcast(I32), words[0].rearrange("p n r -> p (n r)").bitcast(I32))
             return tile
 
         x_bytes = sb.tile([P, T], U8, name="x_bytes")
         d_bytes = sb.tile([P, T], U8, name="d_bytes")
-        d_plane = sb.tile([P, H], U8, name="d_plane", align_bytes=64)
-        for tile in (x_bytes, d_bytes, d_plane):
+        for tile in (x_bytes, d_bytes):
             nc.vector.memset(tile[:].bitcast(I32), 0)
 
+        w1_raw = [load_weight_half("w_raw0", w1, 0, nc.sync)]
+        nc.sync.dma_start(x_bytes[0:P:8, :].bitcast(I32), x_scales[0].bitcast(I32))
         offs_sb = load_list("offs_sb", offs)
+        w1_raw.append(load_weight_half("w_raw1", w1, 1, nc.sync))
+        nc.sync.dma_start(d_bytes[0:P:8, :].bitcast(I32), d_scales[0].bitcast(I32))
         k1_sb = load_list("k1_sb", k1)
+        x_table = load_words("x_table", x_words, nc.sync)
         two_sb = load_list("two_sb", two)
         n1_sb = load_list("n1_sb", n1)
         n2_sb = load_list("n2_sb", n2)
-        n3_sb = load_list("n3_sb", n3)
-        n4_sb = load_list("n4_sb", n4)
-        w1_raw = [load_weight_half("w_raw%d" % half, w1, half, nc.sync) for half in range(2)]
-        x_table = load_words("x_table", x_words, nc.sync)
-        d_table = load_words("d_table", d_words, nc.sync)
-        for j in range(PACK):
-            nc.scalar.dma_start(x_bytes[j:P:32, :].bitcast(I32), x_scales[0, j:16:PACK, :].bitcast(I32))
-        nc.scalar.dma_start(d_bytes[0:P:8, :].bitcast(I32), d_scales[0].bitcast(I32))
         gn_sb = sb.tile([P, PACK], F32, name="gn_sb")
         tau_sb = sb.tile([P, PACK], F32, name="tau_sb")
         nc.gpsimd.dma_start(gn_sb[:], gn.rearrange("(p t) o -> p (t o)", t=PACK))
@@ -73,20 +69,24 @@ def tile_picked_cdjoinpxbrange_none_p_kernel(tc, x_words, x_scales, w1, gn, w2, 
         y_win = [sb.tile([P, WINDOW_ONE], F32, name="y_win%d" % t) for t in range(PACK)]
         b_win = [sb.tile([P, WINDOW_EIGHT], F32, name="b_win%d" % t) for t in range(PACK)]
         a_win = [sb.tile([P, WINDOW_EIGHT], F32, name="a_win%d" % t) for t in range(PACK)]
-        for tile in y_win + b_win + a_win:
+        for tile in y_win + b_win:
             nc.vector.memset(tile[:, S:], 0.0)
+        for tile in a_win:
+            nc.gpsimd.memset(tile[:, S:], 0.0)
 
         def gather_packed(name, table, offsets, dtype):
             tile = sb.tile([P, 16 * offsets.shape[1]], dtype, name=name, align_bytes=64)
             nc.vector.tensor_copy(tile[:], table[:].indirect(offsets[:]))
             return tile
 
-        def deal(name, picked, dtype):
-            tile = sb.tile([P, H], dtype, name=name, align_bytes=64)
+        def deal(dealt, picked):
             nc.vector.tensor_copy(
-                tile[:].rearrange("p (t m) -> p m t", t=PACK), picked[:].rearrange("p (m t) -> p m t", t=PACK)
+                dealt.rearrange("p (t m) -> p m t", t=PACK), picked[:].rearrange("p (m t) -> p m t", t=PACK)
             )
-            return tile
+
+        def place_rows(plane, rows):
+            for j in range(1, PACK):
+                nc.sync.dma_start(plane[j:P:32, :].bitcast(I32), rows[8 * j:P:32, :].bitcast(I32))
 
         def round_weight_half(copy, grouped, raw, half):
             m_half = slice(half * P // 2, (half + 1) * P // 2)
@@ -104,65 +104,95 @@ def tile_picked_cdjoinpxbrange_none_p_kernel(tc, x_words, x_scales, w1, gn, w2, 
         def product(acc, codes, plane, t, rhs_codes, rhs_plane):
             cols = slice(t * P, (t + 1) * P)
             nc.tensor.matmul_mx(acc, lhsT=codes[:, cols].bitcast(FP8X4), lhsT_scale=plane[:, cols],
-                                rhs=rhs_codes[:].bitcast(FP8X4), rhs_scale=rhs_plane[:], start=True, stop=True)
+                                rhs=rhs_codes[:].bitcast(FP8X4), rhs_scale=rhs_plane, start=True, stop=True)
 
-        xq_plane = gather_packed("xq_plane", x_bytes, offs_sb, U8)
-        dk_bytes = gather_packed("dk_bytes", d_bytes, k1_sb, U8)
-        dk_dealt = deal("dk_dealt", dk_bytes, U8)
-        for j in range(PACK):
-            nc.sync.dma_start(d_plane[j:P:32, :].bitcast(I32), dk_dealt[8 * j:P:32, :].bitcast(I32))
-        xt_plane = gather_packed("xt_plane", x_bytes, two_sb, U8)
+        xq_rows = gather_packed("xq_rows", x_bytes, offs_sb, U8)
+        xq_plane = sb.tile([P, S], U8, name="xq_plane", align_bytes=64)
+        nc.vector.tensor_copy(xq_plane[:].bitcast(I32), xq_rows[:].bitcast(I32))
+        place_rows(xq_plane, xq_rows)
+        d_table = load_words("d_table", d_words, nc.sync)
+
+        b_planes = sb.tile([P, H + S], U8, name="b_planes", align_bytes=64)
+        dk_rows = gather_packed("dk_rows", d_bytes, k1_sb, U8)
+        deal(b_planes[:, :H], dk_rows)
 
         w1_grouped = sb.tile([P, PACK * H], BF16, name="w1_grouped", align_bytes=64)
         round_weight_half(nc.scalar.copy, w1_grouped, w1_raw[0], 0)
         round_weight_half(nc.scalar.copy, w1_grouped, w1_raw[1], 1)
-        w2_raw = [load_weight_half("w_raw%d" % half, w2, half, nc.sync) for half in range(2)]
         w1_codes, w1_plane = quantise("w1", w1_grouped, H)
         xq_codes = gather_packed("xq_codes", x_table, offs_sb, U32)
 
         y_bank = [psum.tile([P, 2, S], F32, name="y_bank%d" % u) for u in range(2)]
         for t in range(PACK):
-            product(y_bank[t // 2][:, t % 2, :], w1_codes, w1_plane, t, xq_codes, xq_plane)
+            product(y_bank[t // 2][:, t % 2, :], w1_codes, w1_plane, t, xq_codes, xq_plane[:])
 
+        xt_rows = gather_packed("xt_rows", x_bytes, two_sb, U8)
+        nc.vector.tensor_copy(b_planes[:, H:].bitcast(I32), xt_rows[:].bitcast(I32))
+        place_rows(b_planes, b_planes)
+        w2_raw = [load_weight_half("w_raw%d" % half, w2, half, nc.sync) for half in range(2)]
+        n3_sb = load_list("n3_sb", n3)
+        n4_sb = load_list("n4_sb", n4)
         xt_codes = gather_packed("xt_codes", x_table, two_sb, U32)
         dk_words = gather_packed("dk_words", d_table, k1_sb, U32)
-        d_codes = deal("d_codes", dk_words, U32)
+        d_codes = sb.tile([P, H], U32, name="d_codes", align_bytes=64)
+        deal(d_codes[:], dk_words)
         b_bank = [psum.tile([P, 2, S], F32, name="b_bank%d" % u) for u in range(2)]
         for t in range(PACK):
-            product(b_bank[t // 2][:, t % 2, :], d_codes, d_plane, t, xt_codes, xt_plane)
+            product(b_bank[t // 2][:, t % 2, :], d_codes, b_planes, t, xt_codes, b_planes[:, H:])
 
         pa = sb.tile([P, PACK, S], F32, name="pa")
-        pb = sb.tile([P, PACK, S], F32, name="pb")
-        hi = sb.tile([P, PACK, S], F32, name="hi")
-        lo = sb.tile([P, PACK, S], F32, name="lo")
+        pb_half = sb.tile([P, PACK, S], F32, name="pb_half")
         z_rows = sb.tile([P, PACK, S], BF16, name="z_rows")
         top = sb.tile([P, PACK], F32, name="top")
         shift = sb.tile([P, PACK], F32, name="shift")
-        ea = sb.tile([P, PACK, S], F32, name="ea")
+        ea = [sb.tile([P, S], F32, name="ea%d" % t) for t in range(PACK)]
         w2_grouped = sb.tile([P, PACK * H], BF16, name="w2_grouped", align_bytes=64)
-        for u in range(2):
+
+        def extremes(u, hi_tag, lo_tag):
             pair = slice(2 * u, 2 * u + 2)
             for t in range(2 * u, 2 * u + 2):
                 nc.scalar.copy(y_win[t][:, :S], y_bank[u][:, t % 2, :])
                 nc.scalar.activation(pa[:, t, :], y_win[t][:].indirect(n1_sb[:]), ACT.Copy)
             for t in range(2 * u, 2 * u + 2):
-                nc.scalar.activation(pb[:, t, :], y_win[t][:].indirect(n2_sb[:]), ACT.Copy)
-            nc.vector.tensor_tensor(hi[:, pair, :], y_bank[u][:], pa[:, pair, :], ALU.max)
-            nc.vector.tensor_tensor(lo[:, pair, :], y_bank[u][:], pa[:, pair, :], ALU.min)
-            nc.vector.tensor_tensor(hi[:, pair, :], hi[:, pair, :], pb[:, pair, :], ALU.max)
-            nc.vector.tensor_tensor(lo[:, pair, :], lo[:, pair, :], pb[:, pair, :], ALU.min)
-            for t in range(2 * u, 2 * u + 2):
-                nc.vector.tensor_scalar(b_win[t][:, :S], b_bank[u][:, t % 2, :], 0.0625, None, ALU.mult, ALU.max,
-                                        accum_out=top[:, t:t + 1])
-            nc.vector.scalar_tensor_tensor(hi[:, pair, :], lo[:, pair, :], -0.5, hi[:, pair, :], ALU.mult, ALU.add)
+                nc.scalar.activation(pb_half[:, t, :], y_win[t][:].indirect(n2_sb[:]), ACT.Copy, scale=0.5)
+            hi = sb.tile([P, 2, S], F32, name="hi%d" % u, tag=hi_tag, align_bytes=64)
+            lo = sb.tile([P, 2, S], F32, name="lo%d" % u, tag=lo_tag, align_bytes=64)
+            nc.vector.tensor_tensor(hi[:], y_bank[u][:], pa[:, pair, :], ALU.max)
+            nc.vector.tensor_tensor(lo[:], y_bank[u][:], pa[:, pair, :], ALU.min)
+            nc.vector.scalar_tensor_tensor(hi[:], pb_half[:, pair, :], 2.0, hi[:], ALU.mult, ALU.max)
+            nc.vector.scalar_tensor_tensor(lo[:], lo[:], 0.5, pb_half[:, pair, :], ALU.mult, ALU.min)
+            return hi, lo
+
+        def apply_gain(engine, hi, t):
+            engine.tensor_scalar(z_rows[:, t, :], hi[:, t % 2, :], gn_sb[:, t:t + 1], 0.0, ALU.mult, ALU.add)
+
+        def scale_b(t):
+            nc.vector.tensor_scalar(b_win[t][:, :S], b_bank[t // 2][:, t % 2, :], 0.0625, None, ALU.mult, ALU.max,
+                                    accum_out=top[:, t:t + 1])
+
+        def exp_bias(u):
+            pair = slice(2 * u, 2 * u + 2)
             nc.vector.scalar_tensor_tensor(shift[:, pair], top[:, pair], -1.0, tau_sb[:, pair], ALU.mult, ALU.mult)
-            for t in range(2 * u, 2 * u + 2):
-                nc.vector.tensor_scalar(z_rows[:, t, :], hi[:, t, :], gn_sb[:, t:t + 1], None, ALU.mult)
+
+        hi, lo = extremes(0, "dk_words", "d_table")
+        nc.gpsimd.tensor_tensor(hi[:], hi[:], lo[:], ALU.subtract)
+        apply_gain(nc.gpsimd, hi, 0)
+        apply_gain(nc.gpsimd, hi, 1)
+        scale_b(0)
+        scale_b(1)
+        exp_bias(0)
+        hi, lo = extremes(1, "d_codes", "xt_codes")
+        scale_b(2)
+        nc.vector.tensor_tensor(hi[:], hi[:], lo[:], ALU.subtract)
+        scale_b(3)
+        apply_gain(nc.vector, hi, 2)
+        apply_gain(nc.vector, hi, 3)
+        exp_bias(1)
         for half in range(2):
             round_weight_half(nc.scalar.copy, w2_grouped, w2_raw[half], half)
         w2_codes, w2_plane = quantise("w2", w2_grouped, H)
         for t in range(PACK):
-            nc.scalar.activation(ea[:, t, :], b_win[t][:].indirect(n3_sb[:]), ACT.Exp,
+            nc.scalar.activation(ea[t][:], b_win[t][:].indirect(n3_sb[:]), ACT.Exp,
                                  bias=shift[:, t:t + 1], scale=tau_sb[:, t:t + 1])
 
         z_grouped = sb.tile([P, S * PACK], BF16, name="z_grouped", align_bytes=64)
@@ -170,15 +200,31 @@ def tile_picked_cdjoinpxbrange_none_p_kernel(tc, x_words, x_scales, w1, gn, w2, 
                               z_rows[:].rearrange("p t (c i) -> p c t i", i=4))
         z_codes, z_plane = quantise("z", z_grouped, S)
 
-        out_rows = out.rearrange("(p t) c -> p t c", t=PACK)
+        a_bank = [psum.tile([P, S], F32, name="a_bank%d" % t) for t in range(PACK)]
         for t in range(PACK):
-            a_bank = psum.tile([P, S], F32, name="a_bank%d" % t)
-            product(a_bank[:], w2_codes, w2_plane, t, z_codes, z_plane)
-            nc.scalar.copy(a_win[t][:, :S], a_bank[:])
+            product(a_bank[t][:], w2_codes, w2_plane, t, z_codes, z_plane[:])
+            nc.vector.tensor_copy(a_win[t][:, :S], a_bank[t][:])
+
+        out_rows = out.rearrange("(p t) c -> p t c", t=PACK)
+        term = []
+
+        def difference(t):
             fetched = sb.tile([P, S], F32, name="fetched%d" % t)
-            nc.scalar.activation(fetched[:], a_win[t][:].indirect(n4_sb[:]), ACT.Copy)
-            result = sb.tile([P, S], F32, name="result%d" % t)
-            nc.vector.tensor_tensor(result[:], a_win[t][:, :S], fetched[:], ALU.subtract)
-            nc.vector.scalar_tensor_tensor(result[:], result[:], 2.0, ea[:, t, :], ALU.mult, ALU.mult)
-            nc.vector.scalar_tensor_tensor(result[:], b_win[t][:, :S], -0.5, result[:], ALU.mult, ALU.add)
+            nc.scalar.activation(fetched[:], a_win[t][:].indirect(n4_sb[:]), ACT.Copy, scale=2.0)
+            term.append(sb.tile([P, S], F32, name="term", bufs=3))
+            nc.vector.scalar_tensor_tensor(term[t][:], a_bank[t][:], 2.0, fetched[:], ALU.mult, ALU.subtract)
+            engine = nc.vector if t == PACK - 1 else nc.gpsimd
+            engine.tensor_tensor(term[t][:], term[t][:], ea[t][:], ALU.mult)
+
+        def finish(t, tag):
+            result = sb.tile([P, S], F32, name="result%d" % t, tag=tag)
+            nc.vector.scalar_tensor_tensor(result[:], b_bank[t // 2][:, t % 2, :], -0.03125, term[t][:], ALU.mult, ALU.add)
             nc.sync.dma_start(out_rows[:, t, :], result[:])
+
+        for t in range(3):
+            difference(t)
+        finish(0, "result0")
+        difference(3)
+        finish(1, "result1")
+        finish(2, "ea3")
+        finish(3, "result3")

@@ -71,17 +71,18 @@ def tile_picked_cdjoinpxbrange_none_p_kernel(tc, x_words, x_scales, w1, gn, w2, 
         a_win = [sb.tile([P, WINDOW_EIGHT], F32, name="a_win%d" % t) for t in range(PACK)]
         for tile in y_win + b_win:
             nc.vector.memset(tile[:, S:], 0.0)
-        for tile in a_win:
-            nc.gpsimd.memset(tile[:, S:], 0.0)
+        neg_tau = sb.tile([P, PACK], F32, name="neg_tau")
+        nc.gpsimd.tensor_scalar(neg_tau[:], tau_sb[:], -1.0, 0.0, ALU.mult, ALU.add)
 
         def gather_packed(name, table, offsets, dtype):
             tile = sb.tile([P, 16 * offsets.shape[1]], dtype, name=name, align_bytes=64)
             nc.vector.tensor_copy(tile[:], table[:].indirect(offsets[:]))
             return tile
 
-        def deal(dealt, picked):
+        def deal(dealt, picked, run):
             nc.vector.tensor_copy(
-                dealt.rearrange("p (t m) -> p m t", t=PACK), picked[:].rearrange("p (m t) -> p m t", t=PACK)
+                dealt.rearrange("p (t g i) -> p g t i", t=PACK, i=run),
+                picked[:].rearrange("p (g i t) -> p g t i", t=PACK, i=run),
             )
 
         def place_rows(plane, rows):
@@ -95,8 +96,8 @@ def tile_picked_cdjoinpxbrange_none_p_kernel(tc, x_words, x_scales, w1, gn, w2, 
                 raw[:].rearrange("p j (m t) -> p m j t", t=PACK),
             )
 
-        def quantise(name, grouped, width):
-            codes = sb.tile([P, width], U32, name=name + "_codes", align_bytes=64)
+        def quantise(name, grouped, width, tag):
+            codes = sb.tile([P, width], U32, name=name + "_codes", tag=tag, align_bytes=64)
             plane = sb.tile([P, width], U8, name=name + "_plane", align_bytes=64)
             nc.vector.quantize_mx(codes[:].bitcast(FP8X4), plane[:], grouped[:])
             return codes, plane
@@ -114,12 +115,12 @@ def tile_picked_cdjoinpxbrange_none_p_kernel(tc, x_words, x_scales, w1, gn, w2, 
 
         b_planes = sb.tile([P, H + S], U8, name="b_planes", align_bytes=64)
         dk_rows = gather_packed("dk_rows", d_bytes, k1_sb, U8)
-        deal(b_planes[:, :H], dk_rows)
+        deal(b_planes[:, :H], dk_rows, 16)
 
         w1_grouped = sb.tile([P, PACK * H], BF16, name="w1_grouped", align_bytes=64)
         round_weight_half(nc.scalar.copy, w1_grouped, w1_raw[0], 0)
         round_weight_half(nc.scalar.copy, w1_grouped, w1_raw[1], 1)
-        w1_codes, w1_plane = quantise("w1", w1_grouped, H)
+        w1_codes, w1_plane = quantise("w1", w1_grouped, H, "w1_codes")
         xq_codes = gather_packed("xq_codes", x_table, offs_sb, U32)
 
         y_bank = [psum.tile([P, 2, S], F32, name="y_bank%d" % u) for u in range(2)]
@@ -135,7 +136,7 @@ def tile_picked_cdjoinpxbrange_none_p_kernel(tc, x_words, x_scales, w1, gn, w2, 
         xt_codes = gather_packed("xt_codes", x_table, two_sb, U32)
         dk_words = gather_packed("dk_words", d_table, k1_sb, U32)
         d_codes = sb.tile([P, H], U32, name="d_codes", align_bytes=64)
-        deal(d_codes[:], dk_words)
+        deal(d_codes[:], dk_words, 4)
         b_bank = [psum.tile([P, 2, S], F32, name="b_bank%d" % u) for u in range(2)]
         for t in range(PACK):
             product(b_bank[t // 2][:, t % 2, :], d_codes, b_planes, t, xt_codes, b_planes[:, H:])
@@ -143,9 +144,6 @@ def tile_picked_cdjoinpxbrange_none_p_kernel(tc, x_words, x_scales, w1, gn, w2, 
         pa = sb.tile([P, PACK, S], F32, name="pa")
         pb_half = sb.tile([P, PACK, S], F32, name="pb_half")
         z_rows = sb.tile([P, PACK, S], BF16, name="z_rows")
-        top = sb.tile([P, PACK], F32, name="top")
-        shift = sb.tile([P, PACK], F32, name="shift")
-        ea = [sb.tile([P, S], F32, name="ea%d" % t) for t in range(PACK)]
         w2_grouped = sb.tile([P, PACK * H], BF16, name="w2_grouped", align_bytes=64)
 
         def extremes(u, hi_tag, lo_tag):
@@ -166,39 +164,53 @@ def tile_picked_cdjoinpxbrange_none_p_kernel(tc, x_words, x_scales, w1, gn, w2, 
         def apply_gain(engine, hi, t):
             engine.tensor_scalar(z_rows[:, t, :], hi[:, t % 2, :], gn_sb[:, t:t + 1], 0.0, ALU.mult, ALU.add)
 
-        def scale_b(t):
+        def scale_b(t, top):
             nc.vector.tensor_scalar(b_win[t][:, :S], b_bank[t // 2][:, t % 2, :], 0.0625, None, ALU.mult, ALU.max,
-                                    accum_out=top[:, t:t + 1])
+                                    accum_out=top[:, t % 2:t % 2 + 1])
 
-        def exp_bias(u):
-            pair = slice(2 * u, 2 * u + 2)
-            nc.vector.scalar_tensor_tensor(shift[:, pair], top[:, pair], -1.0, tau_sb[:, pair], ALU.mult, ALU.mult)
+        def exp_bias(engine, u, top):
+            shift = sb.tile([P, 2], F32, name="shift%d" % u)
+            engine.tensor_tensor(shift[:], top[:], neg_tau[:, 2 * u:2 * u + 2], ALU.mult)
+            return shift
+
+        def fetch_ea(t, ea_t, shift):
+            nc.scalar.activation(ea_t, b_win[t][:].indirect(n3_sb[:]), ACT.Exp,
+                                 bias=shift[:, t % 2:t % 2 + 1], scale=tau_sb[:, t:t + 1])
 
         hi, lo = extremes(0, "dk_words", "d_table")
         nc.gpsimd.tensor_tensor(hi[:], hi[:], lo[:], ALU.subtract)
         apply_gain(nc.gpsimd, hi, 0)
         apply_gain(nc.gpsimd, hi, 1)
-        scale_b(0)
-        scale_b(1)
-        exp_bias(0)
+        top = sb.tile([P, 2], F32, name="top0")
+        scale_b(0, top)
+        scale_b(1, top)
+        shift = exp_bias(nc.gpsimd, 0, top)
+        shift = [shift]
         hi, lo = extremes(1, "d_codes", "xt_codes")
-        scale_b(2)
+        top = sb.tile([P, 2], F32, name="top1")
+        scale_b(2, top)
         nc.vector.tensor_tensor(hi[:], hi[:], lo[:], ALU.subtract)
-        scale_b(3)
+        scale_b(3, top)
         apply_gain(nc.vector, hi, 2)
         apply_gain(nc.vector, hi, 3)
-        exp_bias(1)
+        shift.append(exp_bias(nc.gpsimd, 1, top))
         for half in range(2):
             round_weight_half(nc.scalar.copy, w2_grouped, w2_raw[half], half)
-        w2_codes, w2_plane = quantise("w2", w2_grouped, H)
+        w2_codes, w2_plane = quantise("w2", w2_grouped, H, "w2_codes")
         for t in range(PACK):
-            nc.scalar.activation(ea[t][:], b_win[t][:].indirect(n3_sb[:]), ACT.Exp,
-                                 bias=shift[:, t:t + 1], scale=tau_sb[:, t:t + 1])
+            fetch_ea(t, a_win[t][:, S:], shift[t // 2])
 
         z_grouped = sb.tile([P, S * PACK], BF16, name="z_grouped", align_bytes=64)
-        nc.vector.tensor_copy(z_grouped[:].rearrange("p (c i t) -> p c t i", i=4, t=PACK),
-                              z_rows[:].rearrange("p t (c i) -> p c t i", i=4))
-        z_codes, z_plane = quantise("z", z_grouped, S)
+        z_codes = sb.tile([P, S], U32, name="z_codes", align_bytes=64)
+        z_plane = sb.tile([P, S], U8, name="z_plane", align_bytes=64)
+        for half in range(2):
+            quads = slice(half * S // 8, (half + 1) * S // 8)
+            nc.vector.tensor_copy(z_grouped[:].rearrange("p (c i t) -> p c t i", i=4, t=PACK)[:, quads],
+                                  z_rows[:].rearrange("p t (c i) -> p c t i", i=4)[:, quads])
+        for half in range(2):
+            cols = slice(half * S // 2, (half + 1) * S // 2)
+            nc.vector.quantize_mx(z_codes[:, cols].bitcast(FP8X4), z_plane[:, cols],
+                                  z_grouped[:, half * S * 2:(half + 1) * S * 2])
 
         a_bank = [psum.tile([P, S], F32, name="a_bank%d" % t) for t in range(PACK)]
         for t in range(PACK):
@@ -211,20 +223,23 @@ def tile_picked_cdjoinpxbrange_none_p_kernel(tc, x_words, x_scales, w1, gn, w2, 
         def difference(t):
             fetched = sb.tile([P, S], F32, name="fetched%d" % t)
             nc.scalar.activation(fetched[:], a_win[t][:].indirect(n4_sb[:]), ACT.Copy, scale=2.0)
-            term.append(sb.tile([P, S], F32, name="term", bufs=3))
+            term.append(sb.tile([P, S], F32, name="term%d" % t))
             nc.vector.scalar_tensor_tensor(term[t][:], a_bank[t][:], 2.0, fetched[:], ALU.mult, ALU.subtract)
-            engine = nc.vector if t == PACK - 1 else nc.gpsimd
-            engine.tensor_tensor(term[t][:], term[t][:], ea[t][:], ALU.mult)
 
-        def finish(t, tag):
-            result = sb.tile([P, S], F32, name="result%d" % t, tag=tag)
+        def weigh(engine, t):
+            engine.tensor_tensor(term[t][:], term[t][:], a_win[t][:, S:], ALU.mult)
+
+        def finish(t):
+            result = sb.tile([P, S], F32, name="result%d" % t)
             nc.vector.scalar_tensor_tensor(result[:], b_bank[t // 2][:, t % 2, :], -0.03125, term[t][:], ALU.mult, ALU.add)
             nc.sync.dma_start(out_rows[:, t, :], result[:])
 
         for t in range(3):
             difference(t)
-        finish(0, "result0")
+            weigh(nc.gpsimd, t)
         difference(3)
-        finish(1, "result1")
-        finish(2, "ea3")
-        finish(3, "result3")
+        finish(0)
+        finish(1)
+        weigh(nc.vector, 3)
+        finish(2)
+        finish(3)

@@ -18,12 +18,18 @@ K = 512
 H = 512
 S = 256
 T = 2048
-WINDOW_EIGHT = 512
-WINDOW_ONE = 272
+QUADRANT = 32
+BLOCK_PARTITIONS = 8
+LINE_BYTES = 16
+WINDOW_EIGHT = 2 * S
+WINDOW_ONE = S + 16
+B_SCALE = 0.0625
 FLOPS = 3 * 2 * K * H * S
 
 
-def tile_picked_cdjoinpxbrange_none_p_kernel(tc, x_words, x_scales, w1, gn, w2, d_words, d_scales, tau, offs, n1, n2, two, k1, n3, n4, out):
+def tile_picked_cdjoinpxbrange_none_p_kernel(
+    tc, x_words, x_scales, w1, gn, w2, d_words, d_scales, tau, offs, n1, n2, two, k1, n3, n4, out
+):
     nc = tc.nc
     with ExitStack() as ctx:
         lists = ctx.enter_context(tc.tile_pool(name="lists", bufs=1))
@@ -35,94 +41,107 @@ def tile_picked_cdjoinpxbrange_none_p_kernel(tc, x_words, x_scales, w1, gn, w2, 
             nc.sync.dma_start(tile[:], src)
             return tile
 
-        def load_weight_half(name, w, half, queue):
-            tile = sb.tile([P, PACK, H // 2], F32, name=name)
+        def load_weight_half(w, half):
+            tile = sb.tile([P, PACK, H // 2], F32, name="w_raw%d" % half)
             cols = slice(half * H // 2, (half + 1) * H // 2)
-            queue.dma_start(tile[:], w.rearrange("(p j) c -> p j c", j=PACK)[:, :, cols])
+            nc.sync.dma_start(tile[:], w.rearrange("(p j) c -> p j c", j=PACK)[:, :, cols])
             return tile
 
-        def load_words(name, words, queue):
+        def load_words(name, words):
             tile = sb.tile([P, T], U32, name=name, align_bytes=64)
-            queue.dma_start(tile[:].bitcast(I32), words[0].rearrange("p n r -> p (n r)").bitcast(I32))
+            nc.sync.dma_start(tile[:].bitcast(I32), words[0].rearrange("p n r -> p (n r)").bitcast(I32))
             return tile
+
+        def load_scale_rows(tile, scales):
+            nc.sync.dma_start(tile[0:P:BLOCK_PARTITIONS, :].bitcast(I32), scales[0].bitcast(I32))
 
         x_bytes = sb.tile([P, T], U8, name="x_bytes")
         d_bytes = sb.tile([P, T], U8, name="d_bytes")
         for tile in (x_bytes, d_bytes):
             nc.vector.memset(tile[:].bitcast(I32), 0)
 
-        w1_raw = [load_weight_half("w_raw0", w1, 0, nc.sync)]
-        nc.sync.dma_start(x_bytes[0:P:8, :].bitcast(I32), x_scales[0].bitcast(I32))
+        w1_raw = [load_weight_half(w1, 0)]
+        load_scale_rows(x_bytes, x_scales)
         offs_sb = load_list("offs_sb", offs)
-        w1_raw.append(load_weight_half("w_raw1", w1, 1, nc.sync))
-        nc.sync.dma_start(d_bytes[0:P:8, :].bitcast(I32), d_scales[0].bitcast(I32))
+        w1_raw.append(load_weight_half(w1, 1))
+        load_scale_rows(d_bytes, d_scales)
         k1_sb = load_list("k1_sb", k1)
-        x_table = load_words("x_table", x_words, nc.sync)
+        x_table = load_words("x_table", x_words)
         two_sb = load_list("two_sb", two)
         n1_sb = load_list("n1_sb", n1)
         n2_sb = load_list("n2_sb", n2)
-        gn_sb = sb.tile([P, PACK], F32, name="gn_sb")
-        tau_sb = sb.tile([P, PACK], F32, name="tau_sb")
-        nc.gpsimd.dma_start(gn_sb[:], gn.rearrange("(p t) o -> p (t o)", t=PACK))
-        nc.gpsimd.dma_start(tau_sb[:], tau.rearrange("(p t) o -> p (t o)", t=PACK))
 
         y_win = [sb.tile([P, WINDOW_ONE], F32, name="y_win%d" % t) for t in range(PACK)]
         b_win = [sb.tile([P, WINDOW_EIGHT], F32, name="b_win%d" % t) for t in range(PACK)]
         a_win = [sb.tile([P, WINDOW_EIGHT], F32, name="a_win%d" % t) for t in range(PACK)]
         for tile in y_win + b_win:
             nc.vector.memset(tile[:, S:], 0.0)
-        neg_tau = sb.tile([P, PACK], F32, name="neg_tau")
-        nc.gpsimd.tensor_scalar(neg_tau[:], tau_sb[:], -1.0, 0.0, ALU.mult, ALU.add)
 
         def gather_packed(name, table, offsets, dtype):
             tile = sb.tile([P, 16 * offsets.shape[1]], dtype, name=name, align_bytes=64)
             nc.vector.tensor_copy(tile[:], table[:].indirect(offsets[:]))
             return tile
 
-        def deal(dealt, picked, run):
+        def deal(dealt, picked, per_line):
             nc.vector.tensor_copy(
-                dealt.rearrange("p (t g i) -> p g t i", t=PACK, i=run),
-                picked[:].rearrange("p (g i t) -> p g t i", t=PACK, i=run),
+                dealt.rearrange("p (t g i) -> p g t i", t=PACK, i=per_line),
+                picked[:].rearrange("p (g i t) -> p g t i", t=PACK, i=per_line),
             )
 
         def place_rows(plane, rows):
             for j in range(1, PACK):
-                nc.sync.dma_start(plane[j:P:32, :].bitcast(I32), rows[8 * j:P:32, :].bitcast(I32))
+                nc.sync.dma_start(
+                    plane[j:P:QUADRANT, :].bitcast(I32), rows[BLOCK_PARTITIONS * j:P:QUADRANT, :].bitcast(I32)
+                )
 
-        def round_weight_half(copy, grouped, raw, half):
+        def round_weight_half(grouped, raw, half):
             m_half = slice(half * P // 2, (half + 1) * P // 2)
-            copy(
+            nc.scalar.copy(
                 grouped[:].rearrange("p (t m j) -> p m j t", t=PACK, j=PACK)[:, m_half],
                 raw[:].rearrange("p j (m t) -> p m j t", t=PACK),
             )
 
-        def quantise(name, grouped, width, tag):
-            codes = sb.tile([P, width], U32, name=name + "_codes", tag=tag, align_bytes=64)
-            plane = sb.tile([P, width], U8, name=name + "_plane", align_bytes=64)
+        def quantise_weight(name, grouped):
+            codes = sb.tile([P, H], U32, name=name + "_codes", align_bytes=64)
+            plane = sb.tile([P, H], U8, name=name + "_plane", align_bytes=64)
             nc.vector.quantize_mx(codes[:].bitcast(FP8X4), plane[:], grouped[:])
             return codes, plane
 
         def product(acc, codes, plane, t, rhs_codes, rhs_plane):
             cols = slice(t * P, (t + 1) * P)
-            nc.tensor.matmul_mx(acc, lhsT=codes[:, cols].bitcast(FP8X4), lhsT_scale=plane[:, cols],
-                                rhs=rhs_codes[:].bitcast(FP8X4), rhs_scale=rhs_plane, start=True, stop=True)
+            nc.tensor.matmul_mx(
+                acc,
+                lhsT=codes[:, cols].bitcast(FP8X4),
+                lhsT_scale=plane[:, cols],
+                rhs=rhs_codes[:].bitcast(FP8X4),
+                rhs_scale=rhs_plane,
+                start=True,
+                stop=True,
+            )
 
         xq_rows = gather_packed("xq_rows", x_bytes, offs_sb, U8)
         xq_plane = sb.tile([P, S], U8, name="xq_plane", align_bytes=64)
         nc.vector.tensor_copy(xq_plane[:].bitcast(I32), xq_rows[:].bitcast(I32))
         place_rows(xq_plane, xq_rows)
-        d_table = load_words("d_table", d_words, nc.sync)
+        d_table = load_words("d_table", d_words)
+
+        per_row = sb.tile([P, 2, 8], F32, name="per_row", tag="xq_rows", align_bytes=64)
+        gn_sb = per_row[:, 0, :PACK]
+        tau_sb = per_row[:, 1, :PACK]
+        nc.scalar.dma_start(gn_sb, gn.rearrange("(p t) o -> p (t o)", t=PACK))
+        nc.scalar.dma_start(tau_sb, tau.rearrange("(p t) o -> p (t o)", t=PACK))
+        neg_tau = sb.tile([P, PACK], F32, name="neg_tau")
+        nc.gpsimd.tensor_scalar(neg_tau[:], tau_sb, -1.0, 0.0, ALU.mult, ALU.add)
 
         b_planes = sb.tile([P, H + S], U8, name="b_planes", align_bytes=64)
         dk_rows = gather_packed("dk_rows", d_bytes, k1_sb, U8)
-        deal(b_planes[:, :H], dk_rows, 16)
+        deal(b_planes[:, :H], dk_rows, LINE_BYTES)
 
         w1_grouped = sb.tile([P, PACK * H], BF16, name="w1_grouped", align_bytes=64)
-        round_weight_half(nc.scalar.copy, w1_grouped, w1_raw[0], 0)
-        round_weight_half(nc.scalar.copy, w1_grouped, w1_raw[1], 1)
-        w1_codes, w1_plane = quantise("w1", w1_grouped, H, "w1_codes")
+        for half in range(2):
+            round_weight_half(w1_grouped, w1_raw[half], half)
+        w1_codes, w1_plane = quantise_weight("w1", w1_grouped)
         xq_codes = gather_packed("xq_codes", x_table, offs_sb, U32)
-
         y_bank = [psum.tile([P, 2, S], F32, name="y_bank%d" % u) for u in range(2)]
         for t in range(PACK):
             product(y_bank[t // 2][:, t % 2, :], w1_codes, w1_plane, t, xq_codes, xq_plane[:])
@@ -130,13 +149,13 @@ def tile_picked_cdjoinpxbrange_none_p_kernel(tc, x_words, x_scales, w1, gn, w2, 
         xt_rows = gather_packed("xt_rows", x_bytes, two_sb, U8)
         nc.vector.tensor_copy(b_planes[:, H:].bitcast(I32), xt_rows[:].bitcast(I32))
         place_rows(b_planes, b_planes)
-        w2_raw = [load_weight_half("w_raw%d" % half, w2, half, nc.sync) for half in range(2)]
+        w2_raw = [load_weight_half(w2, half) for half in range(2)]
         n3_sb = load_list("n3_sb", n3)
         n4_sb = load_list("n4_sb", n4)
         xt_codes = gather_packed("xt_codes", x_table, two_sb, U32)
         dk_words = gather_packed("dk_words", d_table, k1_sb, U32)
         d_codes = sb.tile([P, H], U32, name="d_codes", align_bytes=64)
-        deal(d_codes[:], dk_words, 4)
+        deal(d_codes[:], dk_words, LINE_BYTES // 4)
         b_bank = [psum.tile([P, 2, S], F32, name="b_bank%d" % u) for u in range(2)]
         for t in range(PACK):
             product(b_bank[t // 2][:, t % 2, :], d_codes, b_planes, t, xt_codes, b_planes[:, H:])
@@ -161,56 +180,62 @@ def tile_picked_cdjoinpxbrange_none_p_kernel(tc, x_words, x_scales, w1, gn, w2, 
             nc.vector.scalar_tensor_tensor(lo[:], lo[:], 0.5, pb_half[:, pair, :], ALU.mult, ALU.min)
             return hi, lo
 
-        def apply_gain(engine, hi, t):
-            engine.tensor_scalar(z_rows[:, t, :], hi[:, t % 2, :], gn_sb[:, t:t + 1], 0.0, ALU.mult, ALU.add)
+        def apply_gain(engine, spread, t):
+            engine.tensor_scalar(z_rows[:, t, :], spread[:, t % 2, :], gn_sb[:, t:t + 1], 0.0, ALU.mult, ALU.add)
 
         def scale_b(t, top):
-            nc.vector.tensor_scalar(b_win[t][:, :S], b_bank[t // 2][:, t % 2, :], 0.0625, None, ALU.mult, ALU.max,
-                                    accum_out=top[:, t % 2:t % 2 + 1])
+            nc.vector.tensor_scalar(
+                b_win[t][:, :S], b_bank[t // 2][:, t % 2, :], B_SCALE, None, ALU.mult, ALU.max,
+                accum_out=top[:, t % 2:t % 2 + 1],
+            )
 
-        def exp_bias(engine, u, top):
+        def exp_bias(u, top):
             shift = sb.tile([P, 2], F32, name="shift%d" % u)
-            engine.tensor_tensor(shift[:], top[:], neg_tau[:, 2 * u:2 * u + 2], ALU.mult)
+            nc.gpsimd.tensor_tensor(shift[:], top[:], neg_tau[:, 2 * u:2 * u + 2], ALU.mult)
             return shift
 
-        def fetch_ea(t, ea_t, shift):
-            nc.scalar.activation(ea_t, b_win[t][:].indirect(n3_sb[:]), ACT.Exp,
-                                 bias=shift[:, t % 2:t % 2 + 1], scale=tau_sb[:, t:t + 1])
+        hi0, lo0 = extremes(0, "dk_words", "d_table")
+        nc.gpsimd.tensor_tensor(hi0[:], hi0[:], lo0[:], ALU.subtract)
+        apply_gain(nc.gpsimd, hi0, 0)
+        apply_gain(nc.gpsimd, hi0, 1)
+        top0 = sb.tile([P, 2], F32, name="top0")
+        scale_b(0, top0)
+        scale_b(1, top0)
+        shifts = [exp_bias(0, top0)]
 
-        hi, lo = extremes(0, "dk_words", "d_table")
-        nc.gpsimd.tensor_tensor(hi[:], hi[:], lo[:], ALU.subtract)
-        apply_gain(nc.gpsimd, hi, 0)
-        apply_gain(nc.gpsimd, hi, 1)
-        top = sb.tile([P, 2], F32, name="top0")
-        scale_b(0, top)
-        scale_b(1, top)
-        shift = exp_bias(nc.gpsimd, 0, top)
-        shift = [shift]
-        hi, lo = extremes(1, "d_codes", "xt_codes")
-        top = sb.tile([P, 2], F32, name="top1")
-        scale_b(2, top)
-        nc.vector.tensor_tensor(hi[:], hi[:], lo[:], ALU.subtract)
-        scale_b(3, top)
-        apply_gain(nc.vector, hi, 2)
-        apply_gain(nc.vector, hi, 3)
-        shift.append(exp_bias(nc.gpsimd, 1, top))
+        hi1, lo1 = extremes(1, "d_codes", "xt_codes")
+        top1 = sb.tile([P, 2], F32, name="top1")
+        scale_b(2, top1)
+        nc.vector.tensor_tensor(hi1[:], hi1[:], lo1[:], ALU.subtract)
+        scale_b(3, top1)
+        apply_gain(nc.vector, hi1, 2)
+        apply_gain(nc.vector, hi1, 3)
+        shifts.append(exp_bias(1, top1))
+
         for half in range(2):
-            round_weight_half(nc.scalar.copy, w2_grouped, w2_raw[half], half)
-        w2_codes, w2_plane = quantise("w2", w2_grouped, H, "w2_codes")
+            round_weight_half(w2_grouped, w2_raw[half], half)
+        w2_codes, w2_plane = quantise_weight("w2", w2_grouped)
+
+        ea = [tile[:, S:] for tile in a_win]
         for t in range(PACK):
-            fetch_ea(t, a_win[t][:, S:], shift[t // 2])
+            nc.scalar.activation(
+                ea[t], b_win[t][:].indirect(n3_sb[:]), ACT.Exp,
+                bias=shifts[t // 2][:, t % 2:t % 2 + 1], scale=tau_sb[:, t:t + 1],
+            )
 
         z_grouped = sb.tile([P, S * PACK], BF16, name="z_grouped", align_bytes=64)
         z_codes = sb.tile([P, S], U32, name="z_codes", align_bytes=64)
         z_plane = sb.tile([P, S], U8, name="z_plane", align_bytes=64)
         for half in range(2):
             quads = slice(half * S // 8, (half + 1) * S // 8)
-            nc.vector.tensor_copy(z_grouped[:].rearrange("p (c i t) -> p c t i", i=4, t=PACK)[:, quads],
-                                  z_rows[:].rearrange("p t (c i) -> p c t i", i=4)[:, quads])
+            nc.vector.tensor_copy(
+                z_grouped[:].rearrange("p (c i t) -> p c t i", i=4, t=PACK)[:, quads],
+                z_rows[:].rearrange("p t (c i) -> p c t i", i=4)[:, quads],
+            )
         for half in range(2):
             cols = slice(half * S // 2, (half + 1) * S // 2)
-            nc.vector.quantize_mx(z_codes[:, cols].bitcast(FP8X4), z_plane[:, cols],
-                                  z_grouped[:, half * S * 2:(half + 1) * S * 2])
+            values = slice(PACK * cols.start, PACK * cols.stop)
+            nc.vector.quantize_mx(z_codes[:, cols].bitcast(FP8X4), z_plane[:, cols], z_grouped[:, values])
 
         a_bank = [psum.tile([P, S], F32, name="a_bank%d" % t) for t in range(PACK)]
         for t in range(PACK):
@@ -227,19 +252,22 @@ def tile_picked_cdjoinpxbrange_none_p_kernel(tc, x_words, x_scales, w1, gn, w2, 
             nc.vector.scalar_tensor_tensor(term[t][:], a_bank[t][:], 2.0, fetched[:], ALU.mult, ALU.subtract)
 
         def weigh(engine, t):
-            engine.tensor_tensor(term[t][:], term[t][:], a_win[t][:, S:], ALU.mult)
+            engine.tensor_tensor(term[t][:], term[t][:], ea[t], ALU.mult)
 
         def finish(t):
             result = sb.tile([P, S], F32, name="result%d" % t)
-            nc.vector.scalar_tensor_tensor(result[:], b_bank[t // 2][:, t % 2, :], -0.03125, term[t][:], ALU.mult, ALU.add)
+            nc.vector.scalar_tensor_tensor(
+                result[:], b_bank[t // 2][:, t % 2, :], -0.5 * B_SCALE, term[t][:], ALU.mult, ALU.add
+            )
             nc.sync.dma_start(out_rows[:, t, :], result[:])
 
-        for t in range(3):
+        last = PACK - 1
+        for t in range(last):
             difference(t)
             weigh(nc.gpsimd, t)
-        difference(3)
-        finish(0)
-        finish(1)
-        weigh(nc.vector, 3)
-        finish(2)
-        finish(3)
+        difference(last)
+        for t in range(last - 1):
+            finish(t)
+        weigh(nc.vector, last)
+        finish(last - 1)
+        finish(last)

from contextlib import ExitStack

import concourse.mybir as mybir

F32 = mybir.dt.float32
BF16 = mybir.dt.bfloat16
I32 = mybir.dt.int32
U32 = mybir.dt.uint32
U16 = mybir.dt.uint16
U8 = mybir.dt.uint8
FP8X4 = mybir.dt.float8_e4m3fn_x4
ALU = mybir.AluOpType
ACT = mybir.ActivationFunctionType

P = 128
PACK = 4
K = 512
H = 512
S = 256
T = 2048
QUADRANT = 32
BLOCK_PARTITIONS = 8
LINE_BYTES = 16
WINDOW_EIGHT = 2 * S
WINDOW_ONE = S + 16
B_SCALE = 0.0625
FLOPS = 3 * 2 * K * H * S


def tile_picked_cdjoinpxbrange_none_p_kernel(
    tc, x_words, x_scales, w1, gn, w2, d_words, d_scales, tau, offs, n1, n2, two, k1, n3, n4, out
):
    nc = tc.nc
    with ExitStack() as ctx:
        lists = ctx.enter_context(tc.tile_pool(name="lists", bufs=1))
        sb = ctx.enter_context(tc.tile_pool(name="sb", bufs=1))
        psum = ctx.enter_context(tc.psum_pool(name="psum", bufs=1))

        def load_list(name, src):
            tile = lists.tile([P, src.shape[1]], U16, name=name)
            nc.sync.dma_start(tile[:], src)
            return tile

        def load_weight_half(w, half):
            tile = sb.tile([P, PACK, H // 2], F32, name="w_raw%d" % half)
            cols = slice(half * H // 2, (half + 1) * H // 2)
            nc.sync.dma_start(tile[:], w.rearrange("(p j) c -> p j c", j=PACK)[:, :, cols])
            return tile

        def load_words(name, words):
            tile = sb.tile([P, T], U32, name=name, align_bytes=64)
            nc.sync.dma_start(tile[:].bitcast(I32), words[0].rearrange("p n r -> p (n r)").bitcast(I32))
            return tile

        def load_scale_rows(tile, scales):
            nc.sync.dma_start(tile[0:P:BLOCK_PARTITIONS, :].bitcast(I32), scales[0].bitcast(I32))

        x_bytes = sb.tile([P, T], U8, name="x_bytes")
        d_bytes = sb.tile([P, T], U8, name="d_bytes")
        for tile in (x_bytes, d_bytes):
            nc.vector.memset(tile[:].bitcast(I32), 0)

        w1_raw = [load_weight_half(w1, 0)]
        load_scale_rows(x_bytes, x_scales)
        offs_sb = load_list("offs_sb", offs)
        w1_raw.append(load_weight_half(w1, 1))
        load_scale_rows(d_bytes, d_scales)
        k1_sb = load_list("k1_sb", k1)
        x_table = load_words("x_table", x_words)
        two_sb = load_list("two_sb", two)
        n1_sb = load_list("n1_sb", n1)
        n2_sb = load_list("n2_sb", n2)

        y_win = [sb.tile([P, WINDOW_ONE], F32, name="y_win%d" % t) for t in range(PACK)]
        b_win = [sb.tile([P, WINDOW_EIGHT], F32, name="b_win%d" % t) for t in range(PACK)]
        a_win = [sb.tile([P, WINDOW_EIGHT], F32, name="a_win%d" % t) for t in range(PACK)]
        for tile in y_win + b_win:
            nc.vector.memset(tile[:, S:], 0.0)

        def gather_packed(name, table, offsets, dtype):
            tile = sb.tile([P, 16 * offsets.shape[1]], dtype, name=name, align_bytes=64)
            nc.vector.tensor_copy(tile[:], table[:].indirect(offsets[:]))
            return tile

        def deal(dealt, picked, per_line):
            nc.vector.tensor_copy(
                dealt.rearrange("p (t g i) -> p g t i", t=PACK, i=per_line),
                picked[:].rearrange("p (g i t) -> p g t i", t=PACK, i=per_line),
            )

        def place_rows(plane, rows):
            for j in range(1, PACK):
                nc.sync.dma_start(
                    plane[j:P:QUADRANT, :].bitcast(I32), rows[BLOCK_PARTITIONS * j:P:QUADRANT, :].bitcast(I32)
                )

        def round_weight_half(grouped, raw, half):
            m_half = slice(half * P // 2, (half + 1) * P // 2)
            nc.scalar.copy(
                grouped[:].rearrange("p (t m j) -> p m j t", t=PACK, j=PACK)[:, m_half],
                raw[:].rearrange("p j (m t) -> p m j t", t=PACK),
            )

        def quantise_weight(name, grouped):
            codes = sb.tile([P, H], U32, name=name + "_codes", align_bytes=64)
            plane = sb.tile([P, H], U8, name=name + "_plane", align_bytes=64)
            nc.vector.quantize_mx(codes[:].bitcast(FP8X4), plane[:], grouped[:])
            return codes, plane

        def product(acc, codes, plane, t, rhs_codes, rhs_plane):
            cols = slice(t * P, (t + 1) * P)
            nc.tensor.matmul_mx(
                acc,
                lhsT=codes[:, cols].bitcast(FP8X4),
                lhsT_scale=plane[:, cols],
                rhs=rhs_codes[:].bitcast(FP8X4),
                rhs_scale=rhs_plane,
                start=True,
                stop=True,
            )

        xq_rows = gather_packed("xq_rows", x_bytes, offs_sb, U8)
        xq_plane = sb.tile([P, S], U8, name="xq_plane", align_bytes=64)
        nc.vector.tensor_copy(xq_plane[:].bitcast(I32), xq_rows[:].bitcast(I32))
        place_rows(xq_plane, xq_rows)
        d_table = load_words("d_table", d_words)

        per_row = sb.tile([P, 2, 8], F32, name="per_row", tag="xq_rows", align_bytes=64)
        gn_sb = per_row[:, 0, :PACK]
        tau_sb = per_row[:, 1, :PACK]
        nc.scalar.dma_start(gn_sb, gn.rearrange("(p t) o -> p (t o)", t=PACK))
        nc.scalar.dma_start(tau_sb, tau.rearrange("(p t) o -> p (t o)", t=PACK))
        neg_tau = sb.tile([P, PACK], F32, name="neg_tau")
        nc.gpsimd.tensor_scalar(neg_tau[:], tau_sb, -1.0, 0.0, ALU.mult, ALU.add)

        b_planes = sb.tile([P, H + S], U8, name="b_planes", align_bytes=64)
        dk_rows = gather_packed("dk_rows", d_bytes, k1_sb, U8)
        deal(b_planes[:, :H], dk_rows, LINE_BYTES)

        w1_grouped = sb.tile([P, PACK * H], BF16, name="w1_grouped", align_bytes=64)
        for half in range(2):
            round_weight_half(w1_grouped, w1_raw[half], half)
        w1_codes, w1_plane = quantise_weight("w1", w1_grouped)
        xq_codes = gather_packed("xq_codes", x_table, offs_sb, U32)
        y_bank = [psum.tile([P, 2, S], F32, name="y_bank%d" % u) for u in range(2)]
        for t in range(PACK):
            product(y_bank[t // 2][:, t % 2, :], w1_codes, w1_plane, t, xq_codes, xq_plane[:])

        xt_rows = gather_packed("xt_rows", x_bytes, two_sb, U8)
        nc.vector.tensor_copy(b_planes[:, H:].bitcast(I32), xt_rows[:].bitcast(I32))
        place_rows(b_planes, b_planes)
        w2_raw = [load_weight_half(w2, half) for half in range(2)]
        n3_sb = load_list("n3_sb", n3)
        n4_sb = load_list("n4_sb", n4)
        xt_codes = gather_packed("xt_codes", x_table, two_sb, U32)
        dk_words = gather_packed("dk_words", d_table, k1_sb, U32)
        d_codes = sb.tile([P, H], U32, name="d_codes", align_bytes=64)
        deal(d_codes[:], dk_words, LINE_BYTES // 4)
        b_bank = [psum.tile([P, 2, S], F32, name="b_bank%d" % u) for u in range(2)]
        for t in range(PACK):
            product(b_bank[t // 2][:, t % 2, :], d_codes, b_planes, t, xt_codes, b_planes[:, H:])

        pa = sb.tile([P, PACK, S], F32, name="pa")
        pb_half = sb.tile([P, PACK, S], F32, name="pb_half")
        z_rows = sb.tile([P, PACK, S], BF16, name="z_rows")
        w2_grouped = sb.tile([P, PACK * H], BF16, name="w2_grouped", align_bytes=64)

        def extremes(u, hi_tag, lo_tag):
            pair = slice(2 * u, 2 * u + 2)
            for t in range(2 * u, 2 * u + 2):
                nc.scalar.copy(y_win[t][:, :S], y_bank[u][:, t % 2, :])
                nc.scalar.activation(pa[:, t, :], y_win[t][:].indirect(n1_sb[:]), ACT.Copy)
            for t in range(2 * u, 2 * u + 2):
                nc.scalar.activation(pb_half[:, t, :], y_win[t][:].indirect(n2_sb[:]), ACT.Copy, scale=0.5)
            hi = sb.tile([P, 2, S], F32, name="hi%d" % u, tag=hi_tag, align_bytes=64)
            lo = sb.tile([P, 2, S], F32, name="lo%d" % u, tag=lo_tag, align_bytes=64)
            nc.vector.tensor_tensor(hi[:], y_bank[u][:], pa[:, pair, :], ALU.max)
            nc.vector.tensor_tensor(lo[:], y_bank[u][:], pa[:, pair, :], ALU.min)
            nc.vector.scalar_tensor_tensor(hi[:], pb_half[:, pair, :], 2.0, hi[:], ALU.mult, ALU.max)
            nc.vector.scalar_tensor_tensor(lo[:], lo[:], 0.5, pb_half[:, pair, :], ALU.mult, ALU.min)
            return hi, lo

        def apply_gain(engine, spread, t):
            engine.tensor_scalar(z_rows[:, t, :], spread[:, t % 2, :], gn_sb[:, t:t + 1], 0.0, ALU.mult, ALU.add)

        def scale_b(t, top):
            nc.vector.tensor_scalar(
                b_win[t][:, :S], b_bank[t // 2][:, t % 2, :], B_SCALE, None, ALU.mult, ALU.max,
                accum_out=top[:, t % 2:t % 2 + 1],
            )

        def exp_bias(u, top):
            shift = sb.tile([P, 2], F32, name="shift%d" % u)
            nc.gpsimd.tensor_tensor(shift[:], top[:], neg_tau[:, 2 * u:2 * u + 2], ALU.mult)
            return shift

        hi0, lo0 = extremes(0, "dk_words", "d_table")
        nc.gpsimd.tensor_tensor(hi0[:], hi0[:], lo0[:], ALU.subtract)
        apply_gain(nc.gpsimd, hi0, 0)
        apply_gain(nc.gpsimd, hi0, 1)
        top0 = sb.tile([P, 2], F32, name="top0")
        scale_b(0, top0)
        scale_b(1, top0)
        shifts = [exp_bias(0, top0)]

        hi1, lo1 = extremes(1, "d_codes", "xt_codes")
        top1 = sb.tile([P, 2], F32, name="top1")
        scale_b(2, top1)
        nc.vector.tensor_tensor(hi1[:], hi1[:], lo1[:], ALU.subtract)
        scale_b(3, top1)
        apply_gain(nc.vector, hi1, 2)
        apply_gain(nc.vector, hi1, 3)
        shifts.append(exp_bias(1, top1))

        for half in range(2):
            round_weight_half(w2_grouped, w2_raw[half], half)
        w2_codes, w2_plane = quantise_weight("w2", w2_grouped)

        ea = [tile[:, S:] for tile in a_win]
        for t in range(PACK):
            nc.scalar.activation(
                ea[t], b_win[t][:].indirect(n3_sb[:]), ACT.Exp,
                bias=shifts[t // 2][:, t % 2:t % 2 + 1], scale=tau_sb[:, t:t + 1],
            )

        z_grouped = sb.tile([P, S * PACK], BF16, name="z_grouped", align_bytes=64)
        z_codes = sb.tile([P, S], U32, name="z_codes", align_bytes=64)
        z_plane = sb.tile([P, S], U8, name="z_plane", align_bytes=64)
        for half in range(2):
            quads = slice(half * S // 8, (half + 1) * S // 8)
            nc.vector.tensor_copy(
                z_grouped[:].rearrange("p (c i t) -> p c t i", i=4, t=PACK)[:, quads],
                z_rows[:].rearrange("p t (c i) -> p c t i", i=4)[:, quads],
            )
        for half in range(2):
            cols = slice(half * S // 2, (half + 1) * S // 2)
            values = slice(PACK * cols.start, PACK * cols.stop)
            nc.vector.quantize_mx(z_codes[:, cols].bitcast(FP8X4), z_plane[:, cols], z_grouped[:, values])

        a_bank = [psum.tile([P, S], F32, name="a_bank%d" % t) for t in range(PACK)]
        for t in range(PACK):
            product(a_bank[t][:], w2_codes, w2_plane, t, z_codes, z_plane[:])
            nc.vector.tensor_copy(a_win[t][:, :S], a_bank[t][:])

        out_rows = out.rearrange("(p t) c -> p t c", t=PACK)
        term = []

        def difference(t):
            fetched = sb.tile([P, S], F32, name="fetched%d" % t)
            nc.scalar.activation(fetched[:], a_win[t][:].indirect(n4_sb[:]), ACT.Copy, scale=2.0)
            term.append(sb.tile([P, S], F32, name="term%d" % t))
            nc.vector.scalar_tensor_tensor(term[t][:], a_bank[t][:], 2.0, fetched[:], ALU.mult, ALU.subtract)

        def weigh(engine, t):
            engine.tensor_tensor(term[t][:], term[t][:], ea[t], ALU.mult)

        def finish(t):
            result = sb.tile([P, S], F32, name="result%d" % t)
            nc.vector.scalar_tensor_tensor(
                result[:], b_bank[t // 2][:, t % 2, :], -0.5 * B_SCALE, term[t][:], ALU.mult, ALU.add
            )
            nc.sync.dma_start(out_rows[:, t, :], result[:])

        last = PACK - 1
        for t in range(last):
            difference(t)
            weigh(nc.gpsimd, t)
        difference(last)
        for t in range(last - 1):
            finish(t)
        weigh(nc.vector, last)
        finish(last - 1)
        finish(last)
